import numpy as np
import ml_dtypes


def mxq(x, axis, fmt="e4m3"):
    dtype, down = {"e4m3": (ml_dtypes.float8_e4m3fn, 7), "e5m2": (ml_dtypes.float8_e5m2, 14)}[fmt]
    v = np.moveaxis(np.asarray(x, np.float32).astype(ml_dtypes.bfloat16).astype(np.float64), axis, -1)
    blocks = v.reshape(v.shape[:-1] + (-1, 32))
    amax = np.abs(blocks).max(-1, keepdims=True)
    byte = np.maximum(np.where(amax > 0, np.frexp(amax)[1] - 1 + 127, 0) - down, 1)
    scale = np.exp2(byte - 127.0)
    codes = (blocks / scale).astype(np.float32).astype(dtype).astype(np.float64)
    return np.moveaxis((codes * scale).reshape(v.shape), -1, axis)


WIDE = False


def mx_kscale(k):
    if not WIDE:
        return np.ones(k)
    levels = np.array([10, -10, 5, -5, 0])
    if k % 512:
        return np.exp2(np.random.permutation(np.resize(levels, k // 32))).repeat(32)
    a = np.empty((k // 512, 16))
    for p in range(k // 512):
        a[p, :8] = np.random.permutation(np.resize(levels, 8))
        for g in range(8):
            far = levels[np.abs(levels - a[p, g]) >= 10]
            a[p, g + 8] = far[np.random.randint(len(far))]
    return np.exp2(a.ravel()).repeat(32)


def f64(x):
    return np.asarray(x).astype(np.float64)


def striped(idx):
    return np.tile(np.asarray(idx).reshape(-1, 16).T, (8, 1)).astype(np.uint16)


def unstriped(offs):
    return offs[:16].T.reshape(-1).astype(np.int64)


E2M1 = np.array([0.0, 0.5, 1.0, 1.5, 2.0, 3.0, 4.0, 6.0, -0.0, -0.5, -1.0, -1.5, -2.0, -3.0, -4.0, -6.0])


def pack_weight(w, fmt):
    k, n = w.shape
    w = f64(np.asarray(w, np.float32).astype(ml_dtypes.bfloat16)).reshape(k // 32, 32, n)
    amax = np.abs(w).max(1)
    if fmt == "e4m3":
        byte = np.frexp(amax)[1] - 1 + 127 - 7
    else:
        mant, ex = np.frexp(amax / 6.0)
        byte = np.where(mant > 0.5, ex, ex - 1) + 127
    byte = np.clip(np.where(amax > 0, byte, 1), 1, 254)
    scaled = (w * np.exp2(127.0 - byte)[:, None, :]).reshape(k, n).astype(np.float32)
    by_word = np.ascontiguousarray(scaled.reshape(k // 512, 128, 4, n).transpose(0, 1, 3, 2))
    if fmt == "e4m3":
        words = by_word.astype(ml_dtypes.float8_e4m3fn).view(np.uint8)
    else:
        c = by_word.astype(ml_dtypes.float4_e2m1fn).view(np.uint8) & 0xF
        words = (c[..., 0::2] | (c[..., 1::2] << 4)).reshape(k // 512, 128, 2 * n)
    return np.ascontiguousarray(words), np.ascontiguousarray(byte.astype(np.uint8).reshape(k // 512, 16, n))


def unpack_weight(words, scales, fmt):
    g, _, n = scales.shape
    words = np.ascontiguousarray(words).reshape(g, 128, n, -1)
    if fmt == "e4m3":
        vals = words.view(ml_dtypes.float8_e4m3fn).astype(np.float64)
    else:
        nib = np.empty((g, 128, n, 4), np.uint8)
        nib[..., 0::2] = words & 0xF
        nib[..., 1::2] = words >> 4
        vals = E2M1[nib]
    vals = vals * np.repeat(np.exp2(scales.astype(np.float64) - 127.0), 8, axis=1)[..., None]
    return vals.transpose(0, 1, 3, 2).reshape(g * 512, n)


K, T, J, R, L, N = 1024, 1024, 384, 512, 512, 256


def setup_inputs():
    n = np.random.standard_normal
    idx = np.random.permutation(T)[:J]
    fk = mx_kscale(K)
    fr = mx_kscale(R)
    fl = mx_kscale(L)
    wp = pack_weight(n((K, R)) * 1 / np.sqrt(K) * fk[:, None] * fr, "e2m1")
    sxp = pack_weight(n((L, J)) / fl[:, None], "e4m3")
    wsp = pack_weight(n((L, R)) * 1 / np.sqrt(L) * fl[:, None] * fr, "e4m3")
    wbp = pack_weight(n((R, N)) * 1 / np.sqrt(R) / fr[:, None], "e2m1")
    return {
        "xf": (n((K, T))).astype(np.float32),
        "fk": (np.random.uniform(0.5, 2.0, (K, 1)) / fk[:, None]).astype(np.float32),
        "w_words": wp[0],
        "w_scales": wp[1],
        "sx_words": sxp[0],
        "sx_scales": sxp[1],
        "ws_words": wsp[0],
        "ws_scales": wsp[1],
        "wb_words": wbp[0],
        "wb_scales": wbp[1],
        "rs": (n((N, J))).astype(np.float32),
        "gm": (np.random.uniform(0.5, 2.0, (N, 1))).astype(np.float32),
        "offs": striped(idx),
    }


def reference(xf, fk, w_words, w_scales, sx_words, sx_scales, ws_words, ws_scales, wb_words, wb_scales, rs, gm, offs):
    idx = unstriped(offs)
    wu = unpack_weight(w_words, w_scales, "e2m1")
    sxu = unpack_weight(sx_words, sx_scales, "e4m3")
    wsu = unpack_weight(ws_words, ws_scales, "e4m3")
    wbu = unpack_weight(wb_words, wb_scales, "e2m1")
    xg = f64(xf)[:, idx]
    x1 = np.pad(xg, ((0, 0), (1, 0)))[:, :J]
    u = (xg - 0.6 * x1) * f64(fk)
    uq = mxq(u, 0, "e4m3")
    a = wu.T @ uq
    b2 = wsu.T @ sxu
    hid = np.maximum(a, b2)
    hidq = mxq(hid, 0, "e4m3")
    p = wbu.T @ hidq
    y = f64(gm) * p + f64(rs)
    return y

@@ -1,0 +1,225 @@
+from contextlib import ExitStack
+
+import concourse.mybir as mybir
+from concourse.masks import make_identity
+
+K, T, J, R, L, N = 1024, 1024, 384, 512, 512, 256
+FLOPS = 2 * J * (K * R + L * R + R * N)
+
+F32 = mybir.dt.float32
+BF16 = mybir.dt.bfloat16
+I32 = mybir.dt.int32
+U32 = mybir.dt.uint32
+U16 = mybir.dt.uint16
+U8 = mybir.dt.uint8
+FP8X4 = mybir.dt.float8_e4m3fn_x4
+FP4X4 = mybir.dt.float4_e2m1fn_x4
+MULT = mybir.AluOpType.mult
+ADD = mybir.AluOpType.add
+MAX = mybir.AluOpType.max
+COPY = mybir.ActivationFunctionType.Copy
+
+P = 128
+PACK = 4
+PASSES = K // (P * PACK)
+CHUNK = 128
+CHUNKS = J // CHUNK
+LEAD = 8
+STEP = 0.6
+
+
+def tile_list_steps_rival_residual_kernel(
+    tc, xf, fk, w_words, w_scales, sx_words, sx_scales, ws_words, ws_scales, wb_words, wb_scales, rs, gm, offs, out
+):
+    nc = tc.nc
+    with ExitStack() as ctx:
+        keep = ctx.enter_context(tc.tile_pool(name="keep", bufs=1))
+        psum = ctx.enter_context(tc.psum_pool(name="psum", bufs=1))
+
+        def held(name, shape, dtype):
+            return keep.tile(shape, dtype, name=name, align_bytes=64)
+
+        offsets = keep.tile([P, J // 16], U16, name="offsets")
+        planes = xf.rearrange("(a p i) t -> a i p t", p=P, i=PACK)
+        window = [[held(f"window{a}{i}", [P, T], F32) for i in range(PACK)] for a in range(PASSES)]
+        fk_sb = held("fk_sb", [P, PASSES, PACK], F32)
+        gm_sb = held("gm_sb", [P, N // P], F32)
+        ws_sb = held("ws_sb", [P, R], U32)
+        sx_sb = held("sx_sb", [P, J], U32)
+        w_sb = [held(f"w_sb{a}", [P, 2 * R], U8) for a in range(PASSES)]
+        wb_sb = held("wb_sb", [P, 2 * N], U8)
+        rs_sb = held("rs_sb", [P, N // P, J], F32)
+
+        def scale_plane(name, scales):
+            passes, rows, width = scales.shape
+            plane = held(name, [P, passes, width], U8)
+            nc.gpsimd.memset(plane[:].bitcast(U32), 0)
+            return plane
+
+        def load_scales(plane, scales):
+            for q in range(4):
+                nc.sync.dma_start(
+                    out=plane[32 * q : 32 * q + 4].bitcast(I32),
+                    in_=scales[:, 4 * q : 4 * q + 4, :].rearrange("a r c -> r a c").bitcast(I32),
+                )
+
+        zeros = held("zeros", [P, 2, 1], F32)
+        nc.vector.memset(zeros[:], 0.0)
+        ws_sc = scale_plane("ws_sc", ws_scales)
+        sx_sc = scale_plane("sx_sc", sx_scales)
+        w_sc = scale_plane("w_sc", w_scales)
+        wb_sc = scale_plane("wb_sc", wb_scales)
+
+        nc.sync.dma_start(out=window[0][0][:], in_=planes[0, 0])
+        nc.sync.dma_start(offsets[:], offs)
+        nc.sync.dma_start(out=fk_sb[:], in_=fk.rearrange("(a p i) o -> p a (i o)", p=P, i=PACK))
+        nc.sync.dma_start(out=window[0][1][:], in_=planes[0, 1])
+        nc.sync.dma_start(out=window[0][2][:], in_=planes[0, 2])
+        load_scales(ws_sc, ws_scales)
+        nc.sync.dma_start(out=window[0][3][:], in_=planes[0, 3])
+        load_scales(sx_sc, sx_scales)
+        nc.sync.dma_start(out=ws_sb[:].bitcast(I32), in_=ws_words[0].rearrange("p c t -> p (c t)").bitcast(I32))
+        nc.sync.dma_start(out=sx_sb[:].bitcast(I32), in_=sx_words[0].rearrange("p c t -> p (c t)").bitcast(I32))
+        nc.sync.dma_start(out=window[1][0][:], in_=planes[1, 0])
+        nc.sync.dma_start(out=window[1][1][:], in_=planes[1, 1])
+        load_scales(w_sc, w_scales)
+        nc.sync.dma_start(out=window[1][2][:], in_=planes[1, 2])
+        nc.sync.dma_start(out=window[1][3][:], in_=planes[1, 3])
+        for a in range(PASSES):
+            nc.sync.dma_start(out=w_sb[a][:].bitcast(I32), in_=w_words[a].bitcast(I32))
+        nc.sync.dma_start(out=wb_sb[:].bitcast(I32), in_=wb_words[0].bitcast(I32))
+        load_scales(wb_sc, wb_scales)
+        with nc.allow_non_contiguous_dma(reason="one factor a partition"):
+            nc.sync.dma_start(out=gm_sb[:], in_=gm.rearrange("(h p) o -> p (h o)", p=P))
+        nc.sync.dma_start(out=rs_sb[:], in_=rs.rearrange("(h p) j -> p h j", p=P))
+
+        ident = held("ident", [P, P], F32)
+        make_identity(nc, ident[:])
+
+        scaled = [[held(f"scaled{a}{h}", [P, 2, LEAD + J], F32) for h in range(2)] for a in range(PASSES)]
+        for a in range(PASSES):
+            for h in range(2):
+                nc.scalar.activation(scaled[a][h][:, :, LEAD - 1 : LEAD], zeros[:], COPY)
+        u_bf = [held(f"u_bf{a}", [P, J, PACK], BF16) for a in range(PASSES)]
+        u_codes = [held(f"u_codes{a}", [P, J], U32) for a in range(PASSES)]
+        u_sc = [held(f"u_sc{a}", [P, J], U8) for a in range(PASSES)]
+
+        def pick(a, i, j0, j1):
+            picked = held(f"picked{a}{i}_{j0}", [P, j1 - j0], F32)
+            nc.scalar.activation(picked[:], window[a][i][:].indirect(offsets[:, j0 // 16 : j1 // 16]), COPY)
+            nc.vector.tensor_scalar(
+                out=scaled[a][i // 2][:, i % 2, LEAD + j0 : LEAD + j1],
+                in0=picked[:],
+                scalar1=fk_sb[:, a, i : i + 1],
+                scalar2=None,
+                op0=MULT,
+            )
+
+        def steps(a, h, j0, j1):
+            src = scaled[a][h]
+            nc.vector.scalar_tensor_tensor(
+                out=u_bf[a][:, j0:j1, 2 * h : 2 * h + 2],
+                in0=src[:, :, LEAD - 1 + j0 : LEAD - 1 + j1].rearrange("p e j -> p j e"),
+                scalar=-STEP,
+                in1=src[:, :, LEAD + j0 : LEAD + j1].rearrange("p e j -> p j e"),
+                op0=MULT,
+                op1=ADD,
+            )
+
+        def quantise_u(a, j0, j1):
+            nc.vector.quantize_mx(
+                out=u_codes[a][:, j0:j1].bitcast(FP8X4),
+                scales=u_sc[a][:, j0:j1],
+                in_=u_bf[a][:, j0:j1, :].rearrange("p j t -> p (j t)"),
+            )
+
+        cols = [slice(c * CHUNK, (c + 1) * CHUNK) for c in range(CHUNKS)]
+        a_ps = [psum.tile([P, R], F32, name=f"a_ps{c}") for c in range(CHUNKS)]
+
+        def first_product(a, c):
+            nc.tensor.matmul_mx(
+                out=a_ps[c][:],
+                lhsT=u_codes[a][:, cols[c]].bitcast(FP8X4),
+                lhsT_scale=u_sc[a][:, cols[c]],
+                rhs=w_sb[a][:].bitcast(FP4X4),
+                rhs_scale=w_sc[:, a, :],
+                start=(a == 0),
+                stop=(a == PASSES - 1),
+            )
+
+        for h in range(2):
+            pick(0, 2 * h, 0, J)
+            pick(0, 2 * h + 1, 0, J)
+            steps(0, h, 0, J)
+        quantise_u(0, 0, J)
+
+        own = []
+        for c in range(CHUNKS):
+            b_ps = psum.tile([P, R], F32, name=f"b_ps{c}", tag=f"turn{c}")
+            nc.tensor.matmul_mx(
+                out=b_ps[:],
+                lhsT=sx_sb[:, cols[c]].bitcast(FP8X4),
+                lhsT_scale=sx_sc[:, 0, cols[c]],
+                rhs=ws_sb[:].bitcast(FP8X4),
+                rhs_scale=ws_sc[:, 0, :],
+                start=True,
+                stop=True,
+            )
+            own_c = held(f"own{c}", [P, 2, P, 2], F32)
+            nc.scalar.copy(out=own_c[:], in_=b_ps[:].rearrange("j (p u e) -> j u p e", u=2, e=2))
+            own.append(own_c)
+
+        pick(1, 0, 0, J)
+        pick(1, 1, 0, J)
+        steps(1, 0, 0, J)
+        pick(1, 2, 0, J)
+        for c in range(CHUNKS):
+            first_product(0, c)
+        for c in range(CHUNKS):
+            pick(1, 3, c * CHUNK, (c + 1) * CHUNK)
+            steps(1, 1, c * CHUNK, (c + 1) * CHUNK)
+            quantise_u(1, c * CHUNK, (c + 1) * CHUNK)
+            first_product(1, c)
+
+        hid_ts = []
+        out_v = out.rearrange("(h p) j -> p h j", p=P)
+        for c in range(CHUNKS):
+            hid_t = held(f"hid_t{c}", [P, 2, P, 2], BF16)
+            nc.vector.tensor_tensor(
+                out=hid_t[:], in0=a_ps[c][:].rearrange("j (p u e) -> j u p e", u=2, e=2), in1=own[c][:], op=MAX
+            )
+            hid_ts.append(hid_t)
+            words = hid_t[:].rearrange("j u p e -> j (u p e)").bitcast(F32)
+            turned = psum.tile([P, 2, CHUNK], F32, name=f"turned{c}", tag=f"turn{c}")
+            for u in range(2):
+                nc.tensor.transpose(turned[:, u, :], words[:, u * P : (u + 1) * P], ident[:])
+            hid_bf = held(f"hid_bf{c}", [P, CHUNK * PACK], BF16)
+            nc.scalar.copy(
+                out=hid_bf[:].bitcast(F32).rearrange("p (j u) -> p j u", u=2),
+                in_=turned[:].rearrange("p u j -> p j u"),
+            )
+            hid_codes = held(f"hid_codes{c}", [P, CHUNK], U32)
+            hid_sc = held(f"hid_sc{c}", [P, CHUNK], U8)
+            nc.vector.quantize_mx(out=hid_codes[:].bitcast(FP8X4), scales=hid_sc[:], in_=hid_bf[:])
+            p_ps = psum.tile([P, N // P, CHUNK], F32, name=f"p_ps{c}", tag=f"p{c % 2}")
+            for h in range(N // P):
+                nc.tensor.matmul_mx(
+                    out=p_ps[:, h, :],
+                    lhsT=wb_sb[:, 2 * P * h : 2 * P * (h + 1)].bitcast(FP4X4),
+                    lhsT_scale=wb_sc[:, 0, P * h : P * (h + 1)],
+                    rhs=hid_codes[:].bitcast(FP8X4),
+                    rhs_scale=hid_sc[:],
+                    start=True,
+                    stop=True,
+                )
+            y = held(f"y{c}", [P, N // P, CHUNK], F32)
+            for h in range(N // P):
+                nc.vector.scalar_tensor_tensor(
+                    out=y[:, h, :],
+                    in0=p_ps[:, h, :],
+                    scalar=gm_sb[:, h : h + 1],
+                    in1=rs_sb[:, h, cols[c]],
+                    op0=MULT,
+                    op1=ADD,
+                )
+            nc.sync.dma_start(out=out_v[:, :, cols[c]], in_=y[:])

@@ -25,6 +25,7 @@ PASSES = K // (P * PACK)
 CHUNK = 128
 CHUNKS = J // CHUNK
 LEAD = 8
+HALO = 32
 STEP = 0.6
 
 
@@ -50,97 +51,97 @@ def tile_list_steps_rival_residual_kernel(
         wb_sb = held("wb_sb", [P, 2 * N], U8)
         rs_sb = held("rs_sb", [P, N // P, J], F32)
 
-        def scale_plane(name, scales):
+        def scale_plane(name, scales, engine):
             passes, rows, width = scales.shape
             plane = held(name, [P, passes, width], U8)
-            nc.gpsimd.memset(plane[:].bitcast(U32), 0)
+            engine.memset(plane[:].bitcast(U32), 0)
             return plane
 
-        def load_scales(plane, scales):
-            for q in range(4):
-                nc.sync.dma_start(
+        def load_scales(queue, plane, scales, quadrants):
+            for q in quadrants:
+                queue.dma_start(
                     out=plane[32 * q : 32 * q + 4].bitcast(I32),
                     in_=scales[:, 4 * q : 4 * q + 4, :].rearrange("a r c -> r a c").bitcast(I32),
                 )
 
         zeros = held("zeros", [P, 2, 1], F32)
         nc.vector.memset(zeros[:], 0.0)
-        ws_sc = scale_plane("ws_sc", ws_scales)
-        sx_sc = scale_plane("sx_sc", sx_scales)
-        w_sc = scale_plane("w_sc", w_scales)
-        wb_sc = scale_plane("wb_sc", wb_scales)
+        ws_sc = scale_plane("ws_sc", ws_scales, nc.gpsimd)
+        sx_sc = scale_plane("sx_sc", sx_scales, nc.gpsimd)
+        w_sc = scale_plane("w_sc", w_scales, nc.vector)
+        wb_sc = scale_plane("wb_sc", wb_scales, nc.vector)
 
         nc.sync.dma_start(out=window[0][0][:], in_=planes[0, 0])
         nc.sync.dma_start(offsets[:], offs)
-        nc.sync.dma_start(out=fk_sb[:], in_=fk.rearrange("(a p i) o -> p a (i o)", p=P, i=PACK))
         nc.sync.dma_start(out=window[0][1][:], in_=planes[0, 1])
+        nc.sync.dma_start(out=fk_sb[:], in_=fk.rearrange("(a p i) o -> p a (i o)", p=P, i=PACK))
         nc.sync.dma_start(out=window[0][2][:], in_=planes[0, 2])
-        load_scales(ws_sc, ws_scales)
+        load_scales(nc.sync, ws_sc, ws_scales, (0, 1))
         nc.sync.dma_start(out=window[0][3][:], in_=planes[0, 3])
-        load_scales(sx_sc, sx_scales)
+        load_scales(nc.sync, ws_sc, ws_scales, (2, 3))
+        nc.sync.dma_start(out=window[1][0][:], in_=planes[1, 0])
+        load_scales(nc.sync, sx_sc, sx_scales, (0, 1))
+        nc.sync.dma_start(out=window[1][1][:], in_=planes[1, 1])
+        load_scales(nc.sync, sx_sc, sx_scales, (2, 3))
+        nc.sync.dma_start(out=window[1][2][:], in_=planes[1, 2])
+        nc.sync.dma_start(out=w_sb[0][:].bitcast(I32), in_=w_words[0].bitcast(I32))
+        nc.sync.dma_start(out=window[1][3][:], in_=planes[1, 3])
         nc.sync.dma_start(out=ws_sb[:].bitcast(I32), in_=ws_words[0].rearrange("p c t -> p (c t)").bitcast(I32))
         nc.sync.dma_start(out=sx_sb[:].bitcast(I32), in_=sx_words[0].rearrange("p c t -> p (c t)").bitcast(I32))
-        nc.sync.dma_start(out=window[1][0][:], in_=planes[1, 0])
-        nc.sync.dma_start(out=window[1][1][:], in_=planes[1, 1])
-        load_scales(w_sc, w_scales)
-        nc.sync.dma_start(out=window[1][2][:], in_=planes[1, 2])
-        nc.sync.dma_start(out=window[1][3][:], in_=planes[1, 3])
-        for a in range(PASSES):
-            nc.sync.dma_start(out=w_sb[a][:].bitcast(I32), in_=w_words[a].bitcast(I32))
+        nc.sync.dma_start(out=w_sb[1][:].bitcast(I32), in_=w_words[1].bitcast(I32))
         nc.sync.dma_start(out=wb_sb[:].bitcast(I32), in_=wb_words[0].bitcast(I32))
-        load_scales(wb_sc, wb_scales)
         with nc.allow_non_contiguous_dma(reason="one factor a partition"):
             nc.sync.dma_start(out=gm_sb[:], in_=gm.rearrange("(h p) o -> p (h o)", p=P))
         nc.sync.dma_start(out=rs_sb[:], in_=rs.rearrange("(h p) j -> p h j", p=P))
+        load_scales(nc.gpsimd, w_sc, w_scales, range(4))
+        load_scales(nc.gpsimd, wb_sc, wb_scales, range(4))
 
         ident = held("ident", [P, P], F32)
         make_identity(nc, ident[:])
 
-        scaled = [[held(f"scaled{a}{h}", [P, 2, LEAD + J], F32) for h in range(2)] for a in range(PASSES)]
-        for a in range(PASSES):
-            for h in range(2):
-                nc.scalar.activation(scaled[a][h][:, :, LEAD - 1 : LEAD], zeros[:], COPY)
-        u_bf = [held(f"u_bf{a}", [P, J, PACK], BF16) for a in range(PASSES)]
-        u_codes = [held(f"u_codes{a}", [P, J], U32) for a in range(PASSES)]
-        u_sc = [held(f"u_sc{a}", [P, J], U8) for a in range(PASSES)]
+        cols = [slice(c * CHUNK, (c + 1) * CHUNK) for c in range(CHUNKS)]
+        scaled = [held(f"scaled{g}", [P, 2, LEAD + J], F32) for g in range(3)]
+        ending = [held(f"ending{c}", [P, 2, HALO + CHUNK], F32) for c in range(CHUNKS)]
+        for g in range(3):
+            nc.scalar.activation(scaled[g][:, :, LEAD - 1 : LEAD], zeros[:], COPY)
+        nc.scalar.activation(ending[0][:, :, HALO - 1 : HALO], zeros[:], COPY)
+        u0_bf = held("u0_bf", [P, J, PACK], BF16)
+        u0_codes = held("u0_codes", [P, J], U32)
+        u0_sc = held("u0_sc", [P, J], U8)
+        u1_bf = [held(f"u1_bf{c}", [P, CHUNK, PACK], BF16) for c in range(CHUNKS)]
+        u1_codes = [held(f"u1_codes{c}", [P, CHUNK], U32) for c in range(CHUNKS)]
+        u1_sc = [held(f"u1_sc{c}", [P, CHUNK], U8) for c in range(CHUNKS)]
 
-        def pick(a, i, j0, j1):
-            picked = held(f"picked{a}{i}_{j0}", [P, j1 - j0], F32)
-            nc.scalar.activation(picked[:], window[a][i][:].indirect(offsets[:, j0 // 16 : j1 // 16]), COPY)
-            nc.vector.tensor_scalar(
-                out=scaled[a][i // 2][:, i % 2, LEAD + j0 : LEAD + j1],
-                in0=picked[:],
-                scalar1=fk_sb[:, a, i : i + 1],
-                scalar2=None,
-                op0=MULT,
-            )
+        def pick(a, i):
+            picked = held(f"picked{a}{i}", [P, J], F32)
+            nc.scalar.activation(picked[:], window[a][i][:].indirect(offsets[:]), COPY)
+            return picked
 
-        def steps(a, h, j0, j1):
-            src = scaled[a][h]
+        def scale(dst, src, a, i):
+            nc.vector.tensor_scalar(out=dst, in0=src, scalar1=fk_sb[:, a, i : i + 1], scalar2=None, op0=MULT)
+
+        def steps(dst, src, first, count):
             nc.vector.scalar_tensor_tensor(
-                out=u_bf[a][:, j0:j1, 2 * h : 2 * h + 2],
-                in0=src[:, :, LEAD - 1 + j0 : LEAD - 1 + j1].rearrange("p e j -> p j e"),
+                out=dst,
+                in0=src[:, :, first - 1 : first - 1 + count].rearrange("p e j -> p j e"),
                 scalar=-STEP,
-                in1=src[:, :, LEAD + j0 : LEAD + j1].rearrange("p e j -> p j e"),
+                in1=src[:, :, first : first + count].rearrange("p e j -> p j e"),
                 op0=MULT,
                 op1=ADD,
             )
 
-        def quantise_u(a, j0, j1):
+        def quantise(codes, scales, values):
             nc.vector.quantize_mx(
-                out=u_codes[a][:, j0:j1].bitcast(FP8X4),
-                scales=u_sc[a][:, j0:j1],
-                in_=u_bf[a][:, j0:j1, :].rearrange("p j t -> p (j t)"),
+                out=codes[:].bitcast(FP8X4), scales=scales[:], in_=values[:].rearrange("p j t -> p (j t)")
             )
 
-        cols = [slice(c * CHUNK, (c + 1) * CHUNK) for c in range(CHUNKS)]
         a_ps = [psum.tile([P, R], F32, name=f"a_ps{c}") for c in range(CHUNKS)]
 
-        def first_product(a, c):
+        def first_product(a, c, codes, scales):
             nc.tensor.matmul_mx(
                 out=a_ps[c][:],
-                lhsT=u_codes[a][:, cols[c]].bitcast(FP8X4),
-                lhsT_scale=u_sc[a][:, cols[c]],
+                lhsT=codes.bitcast(FP8X4),
+                lhsT_scale=scales,
                 rhs=w_sb[a][:].bitcast(FP4X4),
                 rhs_scale=w_sc[:, a, :],
                 start=(a == 0),
@@ -148,12 +149,27 @@ def tile_list_steps_rival_residual_kernel(
             )
 
         for h in range(2):
-            pick(0, 2 * h, 0, J)
-            pick(0, 2 * h + 1, 0, J)
-            steps(0, h, 0, J)
-        quantise_u(0, 0, J)
+            for e in range(2):
+                scale(scaled[h][:, e, LEAD:], pick(0, 2 * h + e)[:], 0, 2 * h + e)
+            steps(u0_bf[:, :, 2 * h : 2 * h + 2], scaled[h], LEAD, J)
+        quantise(u0_codes, u0_sc, u0_bf)
 
-        own = []
+        for e in range(2):
+            scale(scaled[2][:, e, LEAD:], pick(1, e)[:], 1, e)
+        for c in range(CHUNKS):
+            steps(u1_bf[c][:, :, 0:2], scaled[2], LEAD + c * CHUNK, CHUNK)
+        picked = pick(1, 2)
+        for c in range(CHUNKS):
+            back = 1 if c else 0
+            nc.scalar.activation(
+                ending[c][:, 0, HALO - back :],
+                picked[:, c * CHUNK - back : (c + 1) * CHUNK],
+                COPY,
+                scale=fk_sb[:, 1, 2:3],
+            )
+        for c in range(CHUNKS):
+            first_product(0, c, u0_codes[:, cols[c]], u0_sc[:, cols[c]])
+        b_pss = []
         for c in range(CHUNKS):
             b_ps = psum.tile([P, R], F32, name=f"b_ps{c}", tag=f"turn{c}")
             nc.tensor.matmul_mx(
@@ -165,21 +181,30 @@ def tile_list_steps_rival_residual_kernel(
                 start=True,
                 stop=True,
             )
+            b_pss.append(b_ps)
+        last = window[1][3]
+        last_factor = fk_sb[:, 1, 3:4]
+        spread = held("spread", [P, CHUNK], F32)
+        nc.vector.tensor_copy(out=spread[:], in_=last_factor.to_broadcast([P, CHUNK]))
+        for c in range(CHUNKS):
+            if c == 0:
+                entries = offsets[:, 0 : CHUNK // 16]
+                nc.vector.tensor_tensor(ending[0][:, 1, HALO:], last[:].indirect(entries), spread[:], MULT)
+            else:
+                entries = offsets[:, (c * CHUNK - HALO) // 16 : (c + 1) * CHUNK // 16]
+                picked = held(f"picked_last{c}", [P, HALO + CHUNK], F32)
+                nc.scalar.activation(picked[:], last[:].indirect(entries), COPY)
+                nc.scalar.activation(ending[c][:, 1, HALO - 1 :], picked[:, HALO - 1 :], COPY, scale=last_factor)
+            steps(u1_bf[c][:, :, 2:4], ending[c], HALO, CHUNK)
+            quantise(u1_codes[c], u1_sc[c], u1_bf[c])
+            first_product(1, c, u1_codes[c][:], u1_sc[c][:])
+
+        own = []
+        for c in range(CHUNKS):
+            b_ps = b_pss[c]
             own_c = held(f"own{c}", [P, 2, P, 2], F32)
             nc.scalar.copy(out=own_c[:], in_=b_ps[:].rearrange("j (p u e) -> j u p e", u=2, e=2))
             own.append(own_c)
-
-        pick(1, 0, 0, J)
-        pick(1, 1, 0, J)
-        steps(1, 0, 0, J)
-        pick(1, 2, 0, J)
-        for c in range(CHUNKS):
-            first_product(0, c)
-        for c in range(CHUNKS):
-            pick(1, 3, c * CHUNK, (c + 1) * CHUNK)
-            steps(1, 1, c * CHUNK, (c + 1) * CHUNK)
-            quantise_u(1, c * CHUNK, (c + 1) * CHUNK)
-            first_product(1, c)
 
         hid_ts = []
         out_v = out.rearrange("(h p) j -> p h j", p=P)
@@ -189,6 +214,9 @@ def tile_list_steps_rival_residual_kernel(
                 out=hid_t[:], in0=a_ps[c][:].rearrange("j (p u e) -> j u p e", u=2, e=2), in1=own[c][:], op=MAX
             )
             hid_ts.append(hid_t)
+        hid_bfs = []
+        for c in range(CHUNKS):
+            hid_t = hid_ts[c]
             words = hid_t[:].rearrange("j u p e -> j (u p e)").bitcast(F32)
             turned = psum.tile([P, 2, CHUNK], F32, name=f"turned{c}", tag=f"turn{c}")
             for u in range(2):
@@ -198,6 +226,9 @@ def tile_list_steps_rival_residual_kernel(
                 out=hid_bf[:].bitcast(F32).rearrange("p (j u) -> p j u", u=2),
                 in_=turned[:].rearrange("p u j -> p j u"),
             )
+            hid_bfs.append(hid_bf)
+        for c in range(CHUNKS):
+            hid_bf = hid_bfs[c]
             hid_codes = held(f"hid_codes{c}", [P, CHUNK], U32)
             hid_sc = held(f"hid_sc{c}", [P, CHUNK], U8)
             nc.vector.quantize_mx(out=hid_codes[:].bitcast(FP8X4), scales=hid_sc[:], in_=hid_bf[:])
@@ -222,4 +253,8 @@ def tile_list_steps_rival_residual_kernel(
                     op0=MULT,
                     op1=ADD,
                 )
-            nc.sync.dma_start(out=out_v[:, :, cols[c]], in_=y[:])
+            if c < CHUNKS - 1:
+                nc.sync.dma_start(out=out_v[:, :, cols[c]], in_=y[:])
+            else:
+                nc.sync.dma_start(out=out_v[:, 0, cols[c]], in_=y[:, 0, :])
+                nc.scalar.dma_start(out=out_v[:, 1, cols[c]], in_=y[:, 1, :])

@@ -25,7 +25,6 @@ PASSES = K // (P * PACK)
 CHUNK = 128
 CHUNKS = J // CHUNK
 LEAD = 8
-HALO = 32
 STEP = 0.6
 
 
@@ -43,8 +42,8 @@ def tile_list_steps_rival_residual_kernel(
         offsets = keep.tile([P, J // 16], U16, name="offsets")
         planes = xf.rearrange("(a p i) t -> a i p t", p=P, i=PACK)
         window = [[held(f"window{a}{i}", [P, T], F32) for i in range(PACK)] for a in range(PASSES)]
-        fk_sb = held("fk_sb", [P, PASSES, PACK], F32)
-        gm_sb = held("gm_sb", [P, N // P], F32)
+        fk_sb = held("fk_sb", [P, PASSES, 8], F32)
+        gm_sb = held("gm_sb", [P, N // P, 8], F32)
         ws_sb = held("ws_sb", [P, R], U32)
         sx_sb = held("sx_sb", [P, J], U32)
         w_sb = [held(f"w_sb{a}", [P, 2 * R], U8) for a in range(PASSES)]
@@ -69,43 +68,42 @@ def tile_list_steps_rival_residual_kernel(
         ws_sc = scale_plane("ws_sc", ws_scales, nc.gpsimd)
         sx_sc = scale_plane("sx_sc", sx_scales, nc.gpsimd)
         w_sc = scale_plane("w_sc", w_scales, nc.vector)
-        wb_sc = scale_plane("wb_sc", wb_scales, nc.vector)
+        wb_sc = scale_plane("wb_sc", wb_scales, nc.gpsimd)
 
         nc.sync.dma_start(out=window[0][0][:], in_=planes[0, 0])
         nc.sync.dma_start(offsets[:], offs)
         nc.sync.dma_start(out=window[0][1][:], in_=planes[0, 1])
-        nc.sync.dma_start(out=fk_sb[:], in_=fk.rearrange("(a p i) o -> p a (i o)", p=P, i=PACK))
+        nc.sync.dma_start(out=fk_sb[:, :, 0:PACK], in_=fk.rearrange("(a p i) o -> p a (i o)", p=P, i=PACK))
         nc.sync.dma_start(out=window[0][2][:], in_=planes[0, 2])
-        load_scales(nc.sync, ws_sc, ws_scales, (0, 1))
+        load_scales(nc.sync, ws_sc, ws_scales, (0,))
         nc.sync.dma_start(out=window[0][3][:], in_=planes[0, 3])
-        load_scales(nc.sync, ws_sc, ws_scales, (2, 3))
-        nc.sync.dma_start(out=window[1][0][:], in_=planes[1, 0])
-        load_scales(nc.sync, sx_sc, sx_scales, (0, 1))
-        nc.sync.dma_start(out=window[1][1][:], in_=planes[1, 1])
-        load_scales(nc.sync, sx_sc, sx_scales, (2, 3))
-        nc.sync.dma_start(out=window[1][2][:], in_=planes[1, 2])
+        load_scales(nc.sync, ws_sc, ws_scales, (1,))
+        for i in range(3):
+            nc.sync.dma_start(out=window[1][i][:], in_=planes[1, i])
         nc.sync.dma_start(out=w_sb[0][:].bitcast(I32), in_=w_words[0].bitcast(I32))
         nc.sync.dma_start(out=window[1][3][:], in_=planes[1, 3])
+        load_scales(nc.sync, sx_sc, sx_scales, range(4))
         nc.sync.dma_start(out=ws_sb[:].bitcast(I32), in_=ws_words[0].rearrange("p c t -> p (c t)").bitcast(I32))
         nc.sync.dma_start(out=sx_sb[:].bitcast(I32), in_=sx_words[0].rearrange("p c t -> p (c t)").bitcast(I32))
         nc.sync.dma_start(out=w_sb[1][:].bitcast(I32), in_=w_words[1].bitcast(I32))
         nc.sync.dma_start(out=wb_sb[:].bitcast(I32), in_=wb_words[0].bitcast(I32))
-        with nc.allow_non_contiguous_dma(reason="one factor a partition"):
-            nc.sync.dma_start(out=gm_sb[:], in_=gm.rearrange("(h p) o -> p (h o)", p=P))
+        load_scales(nc.sync, wb_sc, wb_scales, range(4))
         nc.sync.dma_start(out=rs_sb[:], in_=rs.rearrange("(h p) j -> p h j", p=P))
+        with nc.allow_non_contiguous_dma(reason="one factor a partition"):
+            nc.sync.dma_start(out=gm_sb[:, :, 0:1], in_=gm.rearrange("(h p) o -> p h o", p=P))
         load_scales(nc.gpsimd, w_sc, w_scales, range(4))
-        load_scales(nc.gpsimd, wb_sc, wb_scales, range(4))
+        load_scales(nc.gpsimd, ws_sc, ws_scales, (2, 3))
 
         ident = held("ident", [P, P], F32)
         make_identity(nc, ident[:])
 
         cols = [slice(c * CHUNK, (c + 1) * CHUNK) for c in range(CHUNKS)]
-        scaled = [held(f"scaled{g}", [P, 2, LEAD + J], F32) for g in range(3)]
-        ending = [held(f"ending{c}", [P, 2, HALO + CHUNK], F32) for c in range(CHUNKS)]
-        for g in range(3):
+        scaled = [held(f"scaled{g}", [P, 2, LEAD + J], F32) for g in range(4)]
+        for g in range(4):
             nc.scalar.activation(scaled[g][:, :, LEAD - 1 : LEAD], zeros[:], COPY)
-        nc.scalar.activation(ending[0][:, :, HALO - 1 : HALO], zeros[:], COPY)
         u0_bf = held("u0_bf", [P, J, PACK], BF16)
+        pairs0 = held("pairs0", [P, 2, J, 2], BF16)
+        pairs1 = [held(f"pairs1_{c}", [P, 2, CHUNK, 2], BF16) for c in range(CHUNKS)]
         u0_codes = held("u0_codes", [P, J], U32)
         u0_sc = held("u0_sc", [P, J], U8)
         u1_bf = [held(f"u1_bf{c}", [P, CHUNK, PACK], BF16) for c in range(CHUNKS)]
@@ -130,12 +128,18 @@ def tile_list_steps_rival_residual_kernel(
                 op1=ADD,
             )
 
+        def weave(dst, pairs):
+            nc.vector.tensor_copy(
+                out=dst[:].rearrange("p j t -> p (j t)").bitcast(I32).rearrange("p (j h) -> p j h", h=2),
+                in_=pairs[:].rearrange("p h j e -> p h (j e)").bitcast(I32).rearrange("p h j -> p j h"),
+            )
+
         def quantise(codes, scales, values):
             nc.vector.quantize_mx(
                 out=codes[:].bitcast(FP8X4), scales=scales[:], in_=values[:].rearrange("p j t -> p (j t)")
             )
 
-        a_ps = [psum.tile([P, R], F32, name=f"a_ps{c}") for c in range(CHUNKS)]
+        a_ps = [psum.tile([P, R], F32, name=f"a_ps{c}", tag=f"sum{c}") for c in range(CHUNKS)]
 
         def first_product(a, c, codes, scales):
             nc.tensor.matmul_mx(
@@ -151,22 +155,15 @@ def tile_list_steps_rival_residual_kernel(
         for h in range(2):
             for e in range(2):
                 scale(scaled[h][:, e, LEAD:], pick(0, 2 * h + e)[:], 0, 2 * h + e)
-            steps(u0_bf[:, :, 2 * h : 2 * h + 2], scaled[h], LEAD, J)
+            steps(pairs0[:, h], scaled[h], LEAD, J)
+        weave(u0_bf, pairs0)
         quantise(u0_codes, u0_sc, u0_bf)
 
         for e in range(2):
             scale(scaled[2][:, e, LEAD:], pick(1, e)[:], 1, e)
         for c in range(CHUNKS):
-            steps(u1_bf[c][:, :, 0:2], scaled[2], LEAD + c * CHUNK, CHUNK)
-        picked = pick(1, 2)
-        for c in range(CHUNKS):
-            back = 1 if c else 0
-            nc.scalar.activation(
-                ending[c][:, 0, HALO - back :],
-                picked[:, c * CHUNK - back : (c + 1) * CHUNK],
-                COPY,
-                scale=fk_sb[:, 1, 2:3],
-            )
+            steps(pairs1[c][:, 0], scaled[2], LEAD + c * CHUNK, CHUNK)
+        nc.scalar.activation(scaled[3][:, 0, LEAD:], pick(1, 2)[:], COPY, scale=fk_sb[:, 1, 2:3])
         for c in range(CHUNKS):
             first_product(0, c, u0_codes[:, cols[c]], u0_sc[:, cols[c]])
         b_pss = []
@@ -187,15 +184,16 @@ def tile_list_steps_rival_residual_kernel(
         spread = held("spread", [P, CHUNK], F32)
         nc.vector.tensor_copy(out=spread[:], in_=last_factor.to_broadcast([P, CHUNK]))
         for c in range(CHUNKS):
+            entries = offsets[:, c * CHUNK // 16 : (c + 1) * CHUNK // 16]
+            dst = scaled[3][:, 1, LEAD + c * CHUNK : LEAD + (c + 1) * CHUNK]
             if c == 0:
-                entries = offsets[:, 0 : CHUNK // 16]
-                nc.vector.tensor_tensor(ending[0][:, 1, HALO:], last[:].indirect(entries), spread[:], MULT)
+                nc.vector.tensor_tensor(dst, last[:].indirect(entries), spread[:], MULT)
             else:
-                entries = offsets[:, (c * CHUNK - HALO) // 16 : (c + 1) * CHUNK // 16]
-                picked = held(f"picked_last{c}", [P, HALO + CHUNK], F32)
+                picked = held(f"picked_last{c}", [P, CHUNK], F32)
                 nc.scalar.activation(picked[:], last[:].indirect(entries), COPY)
-                nc.scalar.activation(ending[c][:, 1, HALO - 1 :], picked[:, HALO - 1 :], COPY, scale=last_factor)
-            steps(u1_bf[c][:, :, 2:4], ending[c], HALO, CHUNK)
+                nc.scalar.activation(dst, picked[:], COPY, scale=last_factor)
+            steps(pairs1[c][:, 1], scaled[3], LEAD + c * CHUNK, CHUNK)
+            weave(u1_bf[c], pairs1[c])
             quantise(u1_codes[c], u1_sc[c], u1_bf[c])
             first_product(1, c, u1_codes[c][:], u1_sc[c][:])
 
@@ -232,7 +230,7 @@ def tile_list_steps_rival_residual_kernel(
             hid_codes = held(f"hid_codes{c}", [P, CHUNK], U32)
             hid_sc = held(f"hid_sc{c}", [P, CHUNK], U8)
             nc.vector.quantize_mx(out=hid_codes[:].bitcast(FP8X4), scales=hid_sc[:], in_=hid_bf[:])
-            p_ps = psum.tile([P, N // P, CHUNK], F32, name=f"p_ps{c}", tag=f"p{c % 2}")
+            p_ps = psum.tile([P, N // P, CHUNK], F32, name=f"p_ps{c}", tag=f"sum{c}")
             for h in range(N // P):
                 nc.tensor.matmul_mx(
                     out=p_ps[:, h, :],
@@ -248,7 +246,7 @@ def tile_list_steps_rival_residual_kernel(
                 nc.vector.scalar_tensor_tensor(
                     out=y[:, h, :],
                     in0=p_ps[:, h, :],
-                    scalar=gm_sb[:, h : h + 1],
+                    scalar=gm_sb[:, h, 0:1],
                     in1=rs_sb[:, h, cols[c]],
                     op0=MULT,
                     op1=ADD,

from contextlib import ExitStack

import concourse.mybir as mybir
from concourse.masks import make_identity

K, T, J, R, L, N = 1024, 1024, 384, 512, 512, 256
FLOPS = 2 * J * (K * R + L * R + R * N)

F32 = mybir.dt.float32
BF16 = mybir.dt.bfloat16
I32 = mybir.dt.int32
U32 = mybir.dt.uint32
U16 = mybir.dt.uint16
U8 = mybir.dt.uint8
FP8X4 = mybir.dt.float8_e4m3fn_x4
FP4X4 = mybir.dt.float4_e2m1fn_x4
MULT = mybir.AluOpType.mult
ADD = mybir.AluOpType.add
MAX = mybir.AluOpType.max
COPY = mybir.ActivationFunctionType.Copy

P = 128
PACK = 4
PASSES = K // (P * PACK)
CHUNK = 128
CHUNKS = J // CHUNK
LEAD = 8
STEP = 0.6


def tile_list_steps_rival_residual_kernel(
    tc, xf, fk, w_words, w_scales, sx_words, sx_scales, ws_words, ws_scales, wb_words, wb_scales, rs, gm, offs, out
):
    nc = tc.nc
    with ExitStack() as ctx:
        keep = ctx.enter_context(tc.tile_pool(name="keep", bufs=1))
        psum = ctx.enter_context(tc.psum_pool(name="psum", bufs=1))

        def held(name, shape, dtype):
            return keep.tile(shape, dtype, name=name, align_bytes=64)

        offsets = keep.tile([P, J // 16], U16, name="offsets")
        planes = xf.rearrange("(a p i) t -> a i p t", p=P, i=PACK)
        window = [[held(f"window{a}{i}", [P, T], F32) for i in range(PACK)] for a in range(PASSES)]
        fk_sb = held("fk_sb", [P, PASSES, 8], F32)
        gm_sb = held("gm_sb", [P, N // P, 8], F32)
        ws_sb = held("ws_sb", [P, R], U32)
        sx_sb = held("sx_sb", [P, J], U32)
        w_sb = [held(f"w_sb{a}", [P, 2 * R], U8) for a in range(PASSES)]
        wb_sb = held("wb_sb", [P, 2 * N], U8)
        rs_sb = held("rs_sb", [P, N // P, J], F32)

        def scale_plane(name, scales, engine):
            passes, rows, width = scales.shape
            plane = held(name, [P, passes, width], U8)
            engine.memset(plane[:].bitcast(U32), 0)
            return plane

        def load_scales(queue, plane, scales, quadrants):
            for q in quadrants:
                queue.dma_start(
                    out=plane[32 * q : 32 * q + 4].bitcast(I32),
                    in_=scales[:, 4 * q : 4 * q + 4, :].rearrange("a r c -> r a c").bitcast(I32),
                )

        zeros = held("zeros", [P, 2, 1], F32)
        nc.vector.memset(zeros[:], 0.0)
        ws_sc = scale_plane("ws_sc", ws_scales, nc.gpsimd)
        sx_sc = scale_plane("sx_sc", sx_scales, nc.gpsimd)
        w_sc = scale_plane("w_sc", w_scales, nc.vector)
        wb_sc = scale_plane("wb_sc", wb_scales, nc.gpsimd)

        nc.sync.dma_start(out=window[0][0][:], in_=planes[0, 0])
        nc.sync.dma_start(offsets[:], offs)
        nc.sync.dma_start(out=window[0][1][:], in_=planes[0, 1])
        nc.sync.dma_start(out=fk_sb[:, :, 0:PACK], in_=fk.rearrange("(a p i) o -> p a (i o)", p=P, i=PACK))
        nc.sync.dma_start(out=window[0][2][:], in_=planes[0, 2])
        load_scales(nc.sync, ws_sc, ws_scales, (0,))
        nc.sync.dma_start(out=window[0][3][:], in_=planes[0, 3])
        load_scales(nc.sync, ws_sc, ws_scales, (1,))
        for i in range(3):
            nc.sync.dma_start(out=window[1][i][:], in_=planes[1, i])
        nc.sync.dma_start(out=w_sb[0][:].bitcast(I32), in_=w_words[0].bitcast(I32))
        nc.sync.dma_start(out=window[1][3][:], in_=planes[1, 3])
        load_scales(nc.sync, sx_sc, sx_scales, range(4))
        nc.sync.dma_start(out=ws_sb[:].bitcast(I32), in_=ws_words[0].rearrange("p c t -> p (c t)").bitcast(I32))
        nc.sync.dma_start(out=sx_sb[:].bitcast(I32), in_=sx_words[0].rearrange("p c t -> p (c t)").bitcast(I32))
        nc.sync.dma_start(out=w_sb[1][:].bitcast(I32), in_=w_words[1].bitcast(I32))
        nc.sync.dma_start(out=wb_sb[:].bitcast(I32), in_=wb_words[0].bitcast(I32))
        load_scales(nc.sync, wb_sc, wb_scales, range(4))
        nc.sync.dma_start(out=rs_sb[:], in_=rs.rearrange("(h p) j -> p h j", p=P))
        with nc.allow_non_contiguous_dma(reason="one factor a partition"):
            nc.sync.dma_start(out=gm_sb[:, :, 0:1], in_=gm.rearrange("(h p) o -> p h o", p=P))
        load_scales(nc.gpsimd, w_sc, w_scales, range(4))
        load_scales(nc.gpsimd, ws_sc, ws_scales, (2, 3))

        ident = held("ident", [P, P], F32)
        make_identity(nc, ident[:])

        cols = [slice(c * CHUNK, (c + 1) * CHUNK) for c in range(CHUNKS)]
        scaled = [held(f"scaled{g}", [P, 2, LEAD + J], F32) for g in range(4)]
        for g in range(4):
            nc.scalar.activation(scaled[g][:, :, LEAD - 1 : LEAD], zeros[:], COPY)
        u0_bf = held("u0_bf", [P, J, PACK], BF16)
        pairs0 = held("pairs0", [P, 2, J, 2], BF16)
        pairs1 = [held(f"pairs1_{c}", [P, 2, CHUNK, 2], BF16) for c in range(CHUNKS)]
        u0_codes = held("u0_codes", [P, J], U32)
        u0_sc = held("u0_sc", [P, J], U8)
        u1_bf = [held(f"u1_bf{c}", [P, CHUNK, PACK], BF16) for c in range(CHUNKS)]
        u1_codes = [held(f"u1_codes{c}", [P, CHUNK], U32) for c in range(CHUNKS)]
        u1_sc = [held(f"u1_sc{c}", [P, CHUNK], U8) for c in range(CHUNKS)]

        def pick(a, i):
            picked = held(f"picked{a}{i}", [P, J], F32)
            nc.scalar.activation(picked[:], window[a][i][:].indirect(offsets[:]), COPY)
            return picked

        def scale(dst, src, a, i):
            nc.vector.tensor_scalar(out=dst, in0=src, scalar1=fk_sb[:, a, i : i + 1], scalar2=None, op0=MULT)

        def steps(dst, src, first, count):
            nc.vector.scalar_tensor_tensor(
                out=dst,
                in0=src[:, :, first - 1 : first - 1 + count].rearrange("p e j -> p j e"),
                scalar=-STEP,
                in1=src[:, :, first : first + count].rearrange("p e j -> p j e"),
                op0=MULT,
                op1=ADD,
            )

        def weave(dst, pairs):
            nc.vector.tensor_copy(
                out=dst[:].rearrange("p j t -> p (j t)").bitcast(I32).rearrange("p (j h) -> p j h", h=2),
                in_=pairs[:].rearrange("p h j e -> p h (j e)").bitcast(I32).rearrange("p h j -> p j h"),
            )

        def quantise(codes, scales, values):
            nc.vector.quantize_mx(
                out=codes[:].bitcast(FP8X4), scales=scales[:], in_=values[:].rearrange("p j t -> p (j t)")
            )

        a_ps = [psum.tile([P, R], F32, name=f"a_ps{c}", tag=f"sum{c}") for c in range(CHUNKS)]

        def first_product(a, c, codes, scales):
            nc.tensor.matmul_mx(
                out=a_ps[c][:],
                lhsT=codes.bitcast(FP8X4),
                lhsT_scale=scales,
                rhs=w_sb[a][:].bitcast(FP4X4),
                rhs_scale=w_sc[:, a, :],
                start=(a == 0),
                stop=(a == PASSES - 1),
            )

        for h in range(2):
            for e in range(2):
                scale(scaled[h][:, e, LEAD:], pick(0, 2 * h + e)[:], 0, 2 * h + e)
            steps(pairs0[:, h], scaled[h], LEAD, J)
        weave(u0_bf, pairs0)
        quantise(u0_codes, u0_sc, u0_bf)

        for e in range(2):
            scale(scaled[2][:, e, LEAD:], pick(1, e)[:], 1, e)
        for c in range(CHUNKS):
            steps(pairs1[c][:, 0], scaled[2], LEAD + c * CHUNK, CHUNK)
        nc.scalar.activation(scaled[3][:, 0, LEAD:], pick(1, 2)[:], COPY, scale=fk_sb[:, 1, 2:3])
        for c in range(CHUNKS):
            first_product(0, c, u0_codes[:, cols[c]], u0_sc[:, cols[c]])
        b_pss = []
        for c in range(CHUNKS):
            b_ps = psum.tile([P, R], F32, name=f"b_ps{c}", tag=f"turn{c}")
            nc.tensor.matmul_mx(
                out=b_ps[:],
                lhsT=sx_sb[:, cols[c]].bitcast(FP8X4),
                lhsT_scale=sx_sc[:, 0, cols[c]],
                rhs=ws_sb[:].bitcast(FP8X4),
                rhs_scale=ws_sc[:, 0, :],
                start=True,
                stop=True,
            )
            b_pss.append(b_ps)
        last = window[1][3]
        last_factor = fk_sb[:, 1, 3:4]
        spread = held("spread", [P, CHUNK], F32)
        nc.vector.tensor_copy(out=spread[:], in_=last_factor.to_broadcast([P, CHUNK]))
        for c in range(CHUNKS):
            entries = offsets[:, c * CHUNK // 16 : (c + 1) * CHUNK // 16]
            dst = scaled[3][:, 1, LEAD + c * CHUNK : LEAD + (c + 1) * CHUNK]
            if c == 0:
                nc.vector.tensor_tensor(dst, last[:].indirect(entries), spread[:], MULT)
            else:
                picked = held(f"picked_last{c}", [P, CHUNK], F32)
                nc.scalar.activation(picked[:], last[:].indirect(entries), COPY)
                nc.scalar.activation(dst, picked[:], COPY, scale=last_factor)
            steps(pairs1[c][:, 1], scaled[3], LEAD + c * CHUNK, CHUNK)
            weave(u1_bf[c], pairs1[c])
            quantise(u1_codes[c], u1_sc[c], u1_bf[c])
            first_product(1, c, u1_codes[c][:], u1_sc[c][:])

        own = []
        for c in range(CHUNKS):
            b_ps = b_pss[c]
            own_c = held(f"own{c}", [P, 2, P, 2], F32)
            nc.scalar.copy(out=own_c[:], in_=b_ps[:].rearrange("j (p u e) -> j u p e", u=2, e=2))
            own.append(own_c)

        hid_ts = []
        out_v = out.rearrange("(h p) j -> p h j", p=P)
        for c in range(CHUNKS):
            hid_t = held(f"hid_t{c}", [P, 2, P, 2], BF16)
            nc.vector.tensor_tensor(
                out=hid_t[:], in0=a_ps[c][:].rearrange("j (p u e) -> j u p e", u=2, e=2), in1=own[c][:], op=MAX
            )
            hid_ts.append(hid_t)
        hid_bfs = []
        for c in range(CHUNKS):
            hid_t = hid_ts[c]
            words = hid_t[:].rearrange("j u p e -> j (u p e)").bitcast(F32)
            turned = psum.tile([P, 2, CHUNK], F32, name=f"turned{c}", tag=f"turn{c}")
            for u in range(2):
                nc.tensor.transpose(turned[:, u, :], words[:, u * P : (u + 1) * P], ident[:])
            hid_bf = held(f"hid_bf{c}", [P, CHUNK * PACK], BF16)
            nc.scalar.copy(
                out=hid_bf[:].bitcast(F32).rearrange("p (j u) -> p j u", u=2),
                in_=turned[:].rearrange("p u j -> p j u"),
            )
            hid_bfs.append(hid_bf)
        for c in range(CHUNKS):
            hid_bf = hid_bfs[c]
            hid_codes = held(f"hid_codes{c}", [P, CHUNK], U32)
            hid_sc = held(f"hid_sc{c}", [P, CHUNK], U8)
            nc.vector.quantize_mx(out=hid_codes[:].bitcast(FP8X4), scales=hid_sc[:], in_=hid_bf[:])
            p_ps = psum.tile([P, N // P, CHUNK], F32, name=f"p_ps{c}", tag=f"sum{c}")
            for h in range(N // P):
                nc.tensor.matmul_mx(
                    out=p_ps[:, h, :],
                    lhsT=wb_sb[:, 2 * P * h : 2 * P * (h + 1)].bitcast(FP4X4),
                    lhsT_scale=wb_sc[:, 0, P * h : P * (h + 1)],
                    rhs=hid_codes[:].bitcast(FP8X4),
                    rhs_scale=hid_sc[:],
                    start=True,
                    stop=True,
                )
            y = held(f"y{c}", [P, N // P, CHUNK], F32)
            for h in range(N // P):
                nc.vector.scalar_tensor_tensor(
                    out=y[:, h, :],
                    in0=p_ps[:, h, :],
                    scalar=gm_sb[:, h, 0:1],
                    in1=rs_sb[:, h, cols[c]],
                    op0=MULT,
                    op1=ADD,
                )
            if c < CHUNKS - 1:
                nc.sync.dma_start(out=out_v[:, :, cols[c]], in_=y[:])
            else:
                nc.sync.dma_start(out=out_v[:, 0, cols[c]], in_=y[:, 0, :])
                nc.scalar.dma_start(out=out_v[:, 1, cols[c]], in_=y[:, 1, :])
